import numpy as np
import ml_dtypes

BF16 = ml_dtypes.bfloat16


def bf(x):
    return np.asarray(x, np.float32).astype(BF16)


def f32(x):
    return np.asarray(x, np.float32)


def f64(x):
    return np.asarray(x).astype(np.float64)


def striped(idx):
    return np.tile(idx.reshape(-1, 16).T, (8, 1))


S, K, M, N, D, V = 1024, 128, 128, 384, 16, 24


def sigmoid(v):
    return 1.0 / (1.0 + np.exp(-v))


def setup_inputs():
    return {"table": bf(np.random.standard_normal((K, S))), "w": bf(np.random.standard_normal((K, M)) / np.sqrt(K)), "b": f32(0.5 * np.random.standard_normal((M, 1))), "offs": striped(np.random.permutation(np.tile(np.arange(S), 2))[:N])}


def reference(table, w, b, offs):
    idx = offs[:16].T.reshape(-1)
    x = f64(table)[:, idx]
    y = f64(w).T @ x
    z = (y + f64(b)) * sigmoid(y + f64(b))
    return z.reshape(M, V, D).max(axis=2)

@@ -1,0 +1,36 @@
+import concourse.mybir as mybir
+
+K, M = 128, 128
+S = 1024
+N = 384
+D = 16
+V = N // D
+
+BF16, F32, U16 = mybir.dt.bfloat16, mybir.dt.float32, mybir.dt.uint16
+
+FLOPS = 2 * K * M * N
+
+
+def tile_gather_matmul_kernel(tc, table, w, b, offs, out):
+    nc = tc.nc
+    with tc.tile_pool(name="held", bufs=1) as held, tc.psum_pool(name="psum", bufs=1) as psum:
+        offsets = held.tile([128, N // 16], U16)
+        nodes = held.tile([K, S], BF16)
+        weights = held.tile([K, M], BF16)
+        bias = held.tile([M, 1], F32)
+        nc.sync.dma_start(nodes[:], table)
+        nc.sync.dma_start(offsets[:], offs)
+        nc.scalar.dma_start(weights[:], w)
+        nc.scalar.dma_start(bias[:], b)
+
+        y = psum.tile([M, N], F32)
+        nc.tensor.matmul(y[:], weights[:], nodes[:].indirect(offsets[:]), start=True, stop=True)
+
+        z = held.tile([M, N], F32)
+        nc.scalar.activation(z[:], y[:], mybir.ActivationFunctionType.Silu, bias=bias[:, 0:1])
+
+        pooled = held.tile([M, V], F32)
+        nc.vector.tensor_reduce(
+            pooled[:], z[:].rearrange("m (v t) -> m v t", t=D), axis=mybir.AxisListType.X, op=mybir.AluOpType.max
+        )
+        nc.sync.dma_start(out, pooled[:])

@@ -23,6 +23,11 @@ def tile_gather_matmul_kernel(tc, table, w, b, offs, out):
         nc.scalar.dma_start(weights[:], w)
         nc.scalar.dma_start(bias[:], b)
 
+        zero = held.tile([M, 1], F32)
+        early = held.tile([M, 1], F32)
+        nc.vector.memset(zero[:], 0.0)
+        nc.scalar.activation(early[:], zero[:], mybir.ActivationFunctionType.Silu)
+
         y = psum.tile([M, N], F32)
         nc.tensor.matmul(y[:], weights[:], nodes[:].indirect(offsets[:]), start=True, stop=True)
 

@@ -5,6 +5,8 @@ S = 1024
 N = 384
 D = 16
 V = N // D
+PIECES = 3
+NP, VP = N // PIECES, V // PIECES
 
 BF16, F32, U16 = mybir.dt.bfloat16, mybir.dt.float32, mybir.dt.uint16
 
@@ -13,7 +15,11 @@ FLOPS = 2 * K * M * N
 
 def tile_gather_matmul_kernel(tc, table, w, b, offs, out):
     nc = tc.nc
-    with tc.tile_pool(name="held", bufs=1) as held, tc.psum_pool(name="psum", bufs=1) as psum:
+    with (
+        tc.tile_pool(name="held", bufs=1) as held,
+        tc.tile_pool(name="ring", bufs=PIECES) as ring,
+        tc.psum_pool(name="psum", bufs=PIECES) as psum,
+    ):
         offsets = held.tile([128, N // 16], U16)
         nodes = held.tile([K, S], BF16)
         weights = held.tile([K, M], BF16)
@@ -28,14 +34,19 @@ def tile_gather_matmul_kernel(tc, table, w, b, offs, out):
         nc.vector.memset(zero[:], 0.0)
         nc.scalar.activation(early[:], zero[:], mybir.ActivationFunctionType.Silu)
 
-        y = psum.tile([M, N], F32)
-        nc.tensor.matmul(y[:], weights[:], nodes[:].indirect(offsets[:]), start=True, stop=True)
-
-        z = held.tile([M, N], F32)
-        nc.scalar.activation(z[:], y[:], mybir.ActivationFunctionType.Silu, bias=bias[:, 0:1])
-
         pooled = held.tile([M, V], F32)
-        nc.vector.tensor_reduce(
-            pooled[:], z[:].rearrange("m (v t) -> m v t", t=D), axis=mybir.AxisListType.X, op=mybir.AluOpType.max
-        )
+        for i in range(PIECES):
+            y = psum.tile([M, NP], F32)
+            picked = nodes[:].indirect(offsets[:, i * NP // 16 : (i + 1) * NP // 16])
+            nc.tensor.matmul(y[:], weights[:], picked, start=True, stop=True)
+
+            z = ring.tile([M, NP], F32)
+            nc.scalar.activation(z[:], y[:], mybir.ActivationFunctionType.Silu, bias=bias[:, 0:1])
+
+            nc.vector.tensor_reduce(
+                pooled[:, i * VP : (i + 1) * VP],
+                z[:].rearrange("m (v t) -> m v t", t=D),
+                axis=mybir.AxisListType.X,
+                op=mybir.AluOpType.max,
+            )
         nc.sync.dma_start(out, pooled[:])

@@ -24,10 +24,10 @@ def tile_gather_matmul_kernel(tc, table, w, b, offs, out):
         nodes = held.tile([K, S], BF16)
         weights = held.tile([K, M], BF16)
         bias = held.tile([M, 1], F32)
-        nc.sync.dma_start(nodes[:], table)
         nc.sync.dma_start(offsets[:], offs)
-        nc.scalar.dma_start(weights[:], w)
-        nc.scalar.dma_start(bias[:], b)
+        nc.scalar.dma_start(nodes[:], table)
+        nc.sync.dma_start(weights[:], w)
+        nc.sync.dma_start(bias[:], b)
 
         zero = held.tile([M, 1], F32)
         early = held.tile([M, 1], F32)

import concourse.mybir as mybir

K, M = 128, 128
S = 1024
N = 384
D = 16
V = N // D
PIECES = 3
NP, VP = N // PIECES, V // PIECES

BF16, F32, U16 = mybir.dt.bfloat16, mybir.dt.float32, mybir.dt.uint16

FLOPS = 2 * K * M * N


def tile_gather_matmul_kernel(tc, table, w, b, offs, out):
    nc = tc.nc
    with (
        tc.tile_pool(name="held", bufs=1) as held,
        tc.tile_pool(name="ring", bufs=PIECES) as ring,
        tc.psum_pool(name="psum", bufs=PIECES) as psum,
    ):
        offsets = held.tile([128, N // 16], U16)
        nodes = held.tile([K, S], BF16)
        weights = held.tile([K, M], BF16)
        bias = held.tile([M, 1], F32)
        nc.sync.dma_start(offsets[:], offs)
        nc.scalar.dma_start(nodes[:], table)
        nc.sync.dma_start(weights[:], w)
        nc.sync.dma_start(bias[:], b)

        zero = held.tile([M, 1], F32)
        early = held.tile([M, 1], F32)
        nc.vector.memset(zero[:], 0.0)
        nc.scalar.activation(early[:], zero[:], mybir.ActivationFunctionType.Silu)

        pooled = held.tile([M, V], F32)
        for i in range(PIECES):
            y = psum.tile([M, NP], F32)
            picked = nodes[:].indirect(offsets[:, i * NP // 16 : (i + 1) * NP // 16])
            nc.tensor.matmul(y[:], weights[:], picked, start=True, stop=True)

            z = ring.tile([M, NP], F32)
            nc.scalar.activation(z[:], y[:], mybir.ActivationFunctionType.Silu, bias=bias[:, 0:1])

            nc.vector.tensor_reduce(
                pooled[:, i * VP : (i + 1) * VP],
                z[:].rearrange("m (v t) -> m v t", t=D),
                axis=mybir.AxisListType.X,
                op=mybir.AluOpType.max,
            )
        nc.sync.dma_start(out, pooled[:])
